import numpy as np
import ml_dtypes


def mxq(x, axis, fmt="e4m3"):
    dtype, down = {"e4m3": (ml_dtypes.float8_e4m3fn, 7), "e5m2": (ml_dtypes.float8_e5m2, 14)}[fmt]
    v = np.moveaxis(np.asarray(x, np.float32).astype(ml_dtypes.bfloat16).astype(np.float64), axis, -1)
    blocks = v.reshape(v.shape[:-1] + (-1, 32))
    amax = np.abs(blocks).max(-1, keepdims=True)
    byte = np.maximum(np.where(amax > 0, np.frexp(amax)[1] - 1 + 127, 0) - down, 1)
    scale = np.exp2(byte - 127.0)
    codes = (blocks / scale).astype(np.float32).astype(dtype).astype(np.float64)
    return np.moveaxis((codes * scale).reshape(v.shape), -1, axis)


WIDE = False


def mx_kscale(k):
    if not WIDE:
        return np.ones(k)
    levels = np.array([10, -10, 5, -5, 0])
    if k % 512:
        return np.exp2(np.random.permutation(np.resize(levels, k // 32))).repeat(32)
    a = np.empty((k // 512, 16))
    for p in range(k // 512):
        a[p, :8] = np.random.permutation(np.resize(levels, 8))
        for g in range(8):
            far = levels[np.abs(levels - a[p, g]) >= 10]
            a[p, g + 8] = far[np.random.randint(len(far))]
    return np.exp2(a.ravel()).repeat(32)


BF16 = ml_dtypes.bfloat16


def bf(x):
    return np.asarray(x, np.float32).astype(BF16)


def f64(x):
    return np.asarray(x).astype(np.float64)


M, K, N, Q = 1024, 1024, 1536, 512


def soft(v, th):
    return np.sign(v) * np.maximum(np.abs(v) - th, 0.0)


def draw0():
    s, t, u = mx_kscale(K), mx_kscale(N), mx_kscale(M)
    return {"x": bf(np.random.standard_normal((M, K)) * s * u[:, None]),
            "b": bf(np.random.standard_normal((K, N)) / np.sqrt(K) / s[:, None] * t),
            "sigma": bf(np.random.uniform(0.4, 0.8, M) * u),
            "lam": bf(np.random.uniform(0.5, 1.5, N) * t),
            "a": bf(np.random.standard_normal((Q, M)) / np.sqrt(M) / u),
            "e": bf((1 + 0.1 * np.random.standard_normal(N)) / t),
            "tau": bf(np.random.uniform(0.1, 0.3, Q)),
            "d": bf(np.random.standard_normal((N, K)) / np.sqrt(N) / t[:, None]),
            "g": bf((1 + 0.1 * np.random.standard_normal(M)) / u),
            "low": bf(0.5 * np.random.standard_normal((M, K)))}


def core(x, b, sigma, lam, a, e, tau, d, g, low):
    y = mxq(f64(x), 1, "e4m3") @ mxq(f64(b), 0, "e4m3")
    z = soft(y, f64(sigma)[:, None] * f64(lam)[None, :])
    c = mxq(f64(a), 1, "e4m3") @ mxq(z, 0, "e4m3")
    code = soft(c * f64(e)[None, :], f64(tau)[:, None])
    r = mxq(z, 1, "e4m3") @ mxq(f64(d), 0, "e4m3")
    clean = f64(low) + f64(g)[:, None] * r
    return code, clean


def e4m3fn_bytes(y):
    return np.clip(np.asarray(y, np.float64), -448.0, 448.0).astype(np.float32).astype(ml_dtypes.float8_e4m3fn).view(np.uint8)


def e4m3fn_values(b):
    return np.asarray(b, np.uint8).view(ml_dtypes.float8_e4m3fn).astype(np.float64)


def setup_inputs():
    d = draw0()
    x0 = np.asarray(d['d']).astype(np.float64)
    s = (np.max(np.abs(x0), axis=(1,), keepdims=True) / 448.0).astype(np.float32)
    out = {}
    for k, v in d.items():
        if k == 'd':
            out['d_bytes'] = e4m3fn_bytes(x0 / s.astype(np.float64))
            out['d_scale'] = s
        else:
            out[k] = v
    return out


def reference(x, b, sigma, lam, a, e, tau, d_bytes, d_scale, g, low):
    return core(x, b, sigma, lam, a, e, tau, e4m3fn_values(d_bytes) * d_scale.astype(np.float64), g, low)

from contextlib import ExitStack

import concourse.mybir as mybir
from concourse.masks import make_identity

M, K, N, Q = 1024, 1024, 1536, 512
FLOPS = 2 * M * N * K + 2 * Q * N * M + 2 * M * K * N

F32 = mybir.dt.float32
BF16 = mybir.dt.bfloat16
U32 = mybir.dt.uint32
U8 = mybir.dt.uint8
FP8 = mybir.dt.float8_e4m3fn
FP8X4 = mybir.dt.float8_e4m3fn_x4
ALU = mybir.AluOpType
ACT = mybir.ActivationFunctionType

P = 128
G = 2
H = 3
C = 2


def tile_two_sided_shrink_transform_f6_kernel(
    tc, x, b, sigma, lam, a, e, tau, d_bytes, d_scale, g, low, code, clean
):
    nc = tc.nc
    ctx = ExitStack()
    with ctx:
        keep = ctx.enter_context(tc.tile_pool(name="keep", bufs=1))
        raw = ctx.enter_context(tc.tile_pool(name="raw", bufs=14))
        work = ctx.enter_context(tc.tile_pool(name="work", bufs=2))
        one = ctx.enter_context(tc.tile_pool(name="one", bufs=1))
        psy = ctx.enter_context(tc.psum_pool(name="psy", bufs=4))
        pst = ctx.enter_context(tc.psum_pool(name="pst", bufs=2))
        psa = ctx.enter_context(tc.psum_pool(name="psa", bufs=2))

        x_v = x.rearrange("(g p t) k -> g p t k", p=P, t=4)
        b_v = b.rearrange("(c p j) n -> c p j n", p=P, j=4)
        d_v = d_bytes.rearrange("(h p t) j -> h p t j", p=P, t=4)
        a_v = a.rearrange("(p i) m -> p i m", i=4)
        low_v = low.rearrange("(g p t) j -> g p t j", p=P, t=4)
        clean_v_ = clean.rearrange("(g p t) j -> g p t j", p=P, t=4)
        code_v_ = code.rearrange("(p i) n -> p i n", i=4)

        ident_f = keep.tile([P, P], F32)
        ident_b = keep.tile([P, P], BF16)
        lam_t = keep.tile([P, N], BF16, align_bytes=64)
        sig_b = keep.tile([P, G, 4], BF16)
        gain_b = keep.tile([P, G, 4], BF16)
        tau_b = keep.tile([P, 4], BF16)
        sig = keep.tile([P, 8], F32)
        gain = keep.tile([P, 8], F32)
        tau_f = keep.tile([P, 4], F32)
        nsig = keep.tile([P, 8], F32)
        ntau = keep.tile([P, 4], F32)
        er = keep.tile([P, P], BF16)
        e_col = keep.tile([P, 12], F32)
        dsc = keep.tile([P, H, 4], F32)
        xq = [keep.tile([P, 2, C, 256], U32, name="xq%d" % i, align_bytes=64) for i in range(G)]
        xs = [keep.tile([P, 2, C, 256], U8, name="xs%d" % i, align_bytes=64) for i in range(G)]
        bq = [keep.tile([P, C, 512], U32, name="bq%d" % i, align_bytes=64) for i in range(H)]
        bs = [keep.tile([P, C, 512], U8, name="bs%d" % i, align_bytes=64) for i in range(H)]
        aq = keep.tile([P, G, 512], U32, align_bytes=64)
        asc = keep.tile([P, G, 512], U8, align_bytes=64)
        dq = [keep.tile([P, 1024], U32, name="dq%d" % i, align_bytes=64) for i in range(H)]
        ds = [keep.tile([P, 1024], U8, name="ds%d" % i, align_bytes=64) for i in range(H)]
        ziq = [keep.tile([P, 512], U32, name="ziq%d" % i, align_bytes=64) for i in range(6)]
        zis = [keep.tile([P, 512], U8, name="zis%d" % i, align_bytes=64) for i in range(6)]

        def load4(src, shape, dt):
            t = raw.tile(shape, dt, name="raw4", align_bytes=64)
            nc.sync.dma_start(out=t[:], in_=src)
            return t

        def load_x(gi, s):
            return load4(x_v[gi][:, 2 * s : 2 * s + 2, :], [P, 2, 1024], BF16)

        def load_b(c, h):
            return load4(b_v[c][:, :, 512 * h : 512 * h + 512], [P, 4, 512], BF16)

        make_identity(nc, ident_f[:])
        make_identity(nc, ident_b[:])
        xr = {}
        br = {}
        xr[0, 0] = load_x(0, 0)
        br[0, 0] = load_b(0, 0)
        br[1, 0] = load_b(1, 0)
        xr[0, 1] = load_x(0, 1)
        nc.gpsimd.dma_start(out=sig_b[:], in_=sigma.rearrange("(g p t) -> p g t", p=P, t=4))
        nc.gpsimd.dma_start(out=gain_b[:], in_=g.rearrange("(g p t) -> p g t", p=P, t=4))
        nc.gpsimd.dma_start(out=tau_b[:], in_=tau.rearrange("(p i) -> p i", i=4))
        nc.gpsimd.dma_start(out=dsc[:], in_=d_scale.rearrange("(h p t) o -> p h (t o)", p=P, t=4))
        nc.vector.memset(er[:], 0.0)
        nc.gpsimd.dma_start(out=er[0:12, :], in_=e.rearrange("(b p) -> b p", p=P))
        nc.sync.dma_start(out=lam_t[:], in_=lam.partition_broadcast(P))
        for h in (1, 2):
            for c in range(C):
                br[c, h] = load_b(c, h)
        xr[1, 0] = load_x(1, 0)
        xr[1, 1] = load_x(1, 1)
        db = [load4(d_v[h], [P, 4, 1024], U8) for h in range(H)]
        ar = [load4(a_v[:, 2 * s : 2 * s + 2, :], [P, 2, 1024], BF16) for s in range(2)]
        low_r = {}
        for gi in range(G):
            for s in range(2):
                low_r[gi, s] = load4(low_v[gi][:, 2 * s : 2 * s + 2, :], [P, 2, 1024], BF16)

        def quant(codes, scales, src):
            nc.vector.quantize_mx(out=codes.bitcast(FP8X4), scales=scales, in_=src)

        def turn_rows(rows, s, dst, engine_copy):
            words = rows[:].bitcast(F32)
            pt = pst.tile([P, 2, 2, P], F32, name="pt")
            for c in range(2):
                for u in range(2):
                    nc.tensor.transpose(pt[:, c, u, :], words[:, s, 256 * c + u : 256 * c + 256 : 2], ident_f[:])
            engine_copy(out=dst.bitcast(F32), in_=pt[:].rearrange("p c u r -> p c r u"))

        def copy_s(out, in_):
            nc.scalar.copy(out=out, in_=in_)

        def copy_v(out, in_):
            nc.vector.tensor_copy(out=out, in_=in_)

        bi = {}

        def b_ilv(c, h, engine_copy):
            bi[c, h] = work.tile([P, 512, 4], BF16, name="bi", align_bytes=64)
            engine_copy(out=bi[c, h][:], in_=br[c, h][:].rearrange("p j n -> p n j"))

        def b_quant(c, h):
            quant(bq[h][:, c, :], bs[h][:, c, :], bi[c, h][:].rearrange("p n j -> p (n j)"))

        ilv8 = {}

        def x_turn(gi, t, engine_copy):
            s, r = t // 2, t % 2
            if r == 0:
                ilv8["x", gi, s] = work.tile([P, 2, 256, 4], BF16, name="xi", align_bytes=64)
            turn_rows(xr[gi, s], r, ilv8["x", gi, s][:, :, P * r : P * r + P, :], engine_copy)

        def x_quant(gi, s):
            src = ilv8["x", gi, s][:].rearrange("p c n t -> p (c n t)")
            quant(xq[gi][:, s, :, :].rearrange("p c n -> p (c n)"), xs[gi][:, s, :, :].rearrange("p c n -> p (c n)"), src)

        def a_turn(i):
            if i == 0:
                ilv8["a"] = work.tile([P, 2, 512, 4], BF16, name="ilv8", align_bytes=64)
            turn_rows(ar[i // 2], i % 2, ilv8["a"][:, :, P * i : P * i + P, :], copy_s)

        def a_quant():
            src = ilv8["a"][:].rearrange("p c n t -> p (c n t)")
            quant(aq[:].rearrange("p c n -> p (c n)"), asc[:].rearrange("p c n -> p (c n)"), src)

        dw = {}

        def d_widen(h, t):
            if t == 0:
                dw[h] = one.tile([P, 4, 1024], BF16, name="dw", align_bytes=64)
            nc.scalar.activation(out=dw[h][:, t, :], in_=db[h][:, t, :].bitcast(FP8), func=ACT.Copy, scale=dsc[:, h, t : t + 1])

        def d_ilv(h, s, engine_copy):
            if s == 0:
                ilv8["d", h] = work.tile([P, 1024, 4], BF16, name="ilv8", align_bytes=64)
            cols = slice(512 * s, 512 * s + 512)
            engine_copy(out=ilv8["d", h][:, cols, :], in_=dw[h][:, :, cols].rearrange("p t j -> p j t"))

        def d_quant(h):
            quant(dq[h][:], ds[h][:], ilv8["d", h][:].rearrange("p j t -> p (j t)"))

        chunks = [(gi, h) for gi in range(G) for h in range(H)]
        ybank = {}

        def y_mm(k, t):
            gi, h = chunks[k]
            acc = psy.tile([P, 512], F32, name="y")
            rows = slice(P * (t % 2), P * (t % 2) + P)
            for c in range(C):
                nc.tensor.matmul_mx(
                    out=acc[:],
                    lhsT=xq[gi][:, t // 2, c, rows].bitcast(FP8X4),
                    lhsT_scale=xs[gi][:, t // 2, c, rows],
                    rhs=bq[h][:, c, :].bitcast(FP8X4),
                    rhs_scale=bs[h][:, c, :],
                    start=(c == 0),
                    stop=(c == C - 1),
                )
            ybank[k, t] = acc

        hi = {}
        lo = {}

        def soft_ab(k, t):
            gi, h = chunks[k]
            if t == 0:
                hi[k] = one.tile([P, 4, 512], F32, name="hi")
                lo[k] = one.tile([P, 4, 512], F32, name="lo")
            lam_h = lam_t[:, 512 * h : 512 * h + 512]
            col = slice(4 * gi + t, 4 * gi + t + 1)
            nc.vector.scalar_tensor_tensor(out=hi[k][:, t, :], in0=lam_h, scalar=sig[:, col], in1=ybank[k, t][:], op0=ALU.mult, op1=ALU.add)
            nc.vector.scalar_tensor_tensor(out=lo[k][:, t, :], in0=lam_h, scalar=nsig[:, col], in1=ybank[k, t][:], op0=ALU.mult, op1=ALU.add)

        zi = {}

        def soft_z(k):
            zi[k] = work.tile([P, 512, 4], BF16, name="zi", align_bytes=64)
            nc.vector.scalar_tensor_tensor(
                out=zi[k][:],
                in0=hi[k][:].rearrange("p t n -> p n t"),
                scalar=0.0,
                in1=lo[k][:].rearrange("p t n -> p n t"),
                op0=ALU.min,
                op1=ALU.max,
            )

        def zi_quant(k):
            quant(ziq[k][:], zis[k][:], zi[k][:].rearrange("p n t -> p (n t)"))

        zt = {}

        def z_turn(k, t):
            if t == 0:
                zt[k] = work.tile([P, 512, 4], BF16, name="zt", align_bytes=64)
            pt = pst.tile([P, 4, P], BF16, name="pt")
            zv = zi[k][:].rearrange("p (q s) t -> p s t q", s=4)
            for s in range(4):
                nc.tensor.transpose(pt[:, s, :], zv[:, s, t, :], ident_b[:])
            copy_s(out=zt[k][:, P * t : P * t + P, :], in_=pt[:].rearrange("q s p -> q p s"))

        ztq = {}
        zts = {}

        def zt_quant(k):
            ztq[k] = work.tile([P, 512], U32, name="ztq", bufs=4, align_bytes=64)
            zts[k] = work.tile([P, 512], U8, name="zts", bufs=4, align_bytes=64)
            quant(ztq[k][:], zts[k][:], zt[k][:].rearrange("p n s -> p (n s)"))

        cacc = {}
        co = {}

        def clean_mm(gi, j, hs, pool=None, name="acc"):
            t, s = j // 2, j % 2
            cols = slice(512 * s, 512 * s + 512)
            if hs[0] == 0:
                cacc[gi, j] = (pool or psa).tile([P, 512], F32, name=name)
            for h in hs:
                k = H * gi + h
                nc.tensor.matmul_mx(
                    out=cacc[gi, j][:],
                    lhsT=ztq[k][:, P * t : P * t + P].bitcast(FP8X4),
                    lhsT_scale=zts[k][:, P * t : P * t + P],
                    rhs=dq[h][:, cols].bitcast(FP8X4),
                    rhs_scale=ds[h][:, cols],
                    start=(h == 0),
                    stop=(h == H - 1),
                )

        def clean_v(gi, j):
            t, s = j // 2, j % 2
            cols = slice(512 * s, 512 * s + 512)
            if s == 0:
                co[gi, t] = work.tile([P, 1024], F32, name="o", bufs=3)
            nc.vector.scalar_tensor_tensor(
                out=co[gi, t][:, cols],
                in0=cacc[gi, j][:],
                scalar=gain[:, 4 * gi + t : 4 * gi + t + 1],
                in1=low_r[gi, t // 2][:, t % 2, cols],
                op0=ALU.mult,
                op1=ALU.add,
            )
            if s == 1:
                nc.sync.dma_start(out=clean_v_[gi][:, t, :], in_=co[gi, t][:])

        ce = {}

        def code_mm(h, nb):
            acc = psa.tile([P, 512], F32, name="acc")
            cols = slice(P * nb, P * nb + P)
            for gi in range(G):
                k = H * gi + h
                nc.tensor.matmul_mx(
                    out=acc[:],
                    lhsT=ziq[k][:, cols].bitcast(FP8X4),
                    lhsT_scale=zis[k][:, cols],
                    rhs=aq[:, gi, :].bitcast(FP8X4),
                    rhs_scale=asc[:, gi, :],
                    start=(gi == 0),
                    stop=(gi == G - 1),
                )
            if nb == 0:
                ce[h] = one.tile([P, 4, 512], F32, name="ce")
            nc.scalar.activation(out=ce[h][:, nb, :], in_=acc[:], func=ACT.Copy, scale=e_col[:, 4 * h + nb : 4 * h + nb + 1])

        cpt = {}
        cu = {}

        def code_turn(h, i):
            pt = pst.tile([P, 4, P], F32, name="pt")
            for nb in range(4):
                nc.tensor.transpose(pt[:, nb, :], ce[h][:, nb, P * i : P * i + P], ident_f[:])
            cpt[h, i] = pt[:].rearrange("p b n -> p (b n)")
            cu[h, i] = work.tile([P, 512], F32, name="u")
            nc.scalar.activation(out=cu[h, i][:], in_=cpt[h, i], func=ACT.Relu, bias=ntau[:, i : i + 1])

        def code_v(h, i):
            o = work.tile([P, 512], F32, name="co", bufs=3)
            nc.vector.scalar_tensor_tensor(out=o[:], in0=cpt[h, i], scalar=tau_f[:, i : i + 1], in1=cu[h, i][:], op0=ALU.add, op1=ALU.min)
            nc.sync.dma_start(out=code_v_[:, i, 512 * h : 512 * h + 512], in_=o[:])

        nc.vector.tensor_copy(out=sig[:], in_=sig_b[:].rearrange("p g t -> p (g t)"))
        nc.vector.tensor_copy(out=gain[:], in_=gain_b[:].rearrange("p g t -> p (g t)"))
        nc.vector.tensor_copy(out=tau_f[:], in_=tau_b[:])
        nc.vector.tensor_scalar(out=nsig[:], in0=sig_b[:].rearrange("p g t -> p (g t)"), scalar1=-1.0, scalar2=None, op0=ALU.mult)
        nc.vector.tensor_scalar(out=ntau[:], in0=tau_b[:], scalar1=-1.0, scalar2=None, op0=ALU.mult)
        x_turn(0, 0, copy_s)
        x_turn(0, 1, copy_s)
        b_ilv(0, 0, copy_v)
        b_quant(0, 0)
        x_quant(0, 0)
        b_ilv(1, 0, copy_v)
        b_quant(1, 0)
        x_turn(0, 2, copy_s)
        x_turn(0, 3, copy_s)
        y_mm(0, 0)
        y_mm(0, 1)
        et = pst.tile([P, P], BF16, name="pt")
        nc.tensor.transpose(et[:], er[:], ident_b[:])
        nc.scalar.copy(out=e_col[:], in_=et[:, 0:12])
        b_ilv(0, 1, copy_s)
        b_ilv(1, 1, copy_s)

        plan = {
            (0, 0): [(x_quant, 0, 1), (y_mm, 0, 2), (y_mm, 0, 3)],
            (0, 1): [(b_ilv, 0, 2, copy_s)],
            (0, 2): [(b_quant, 0, 1)],
            (0, 3): [(b_quant, 1, 1), (y_mm, 1, 0), (y_mm, 1, 1), (y_mm, 1, 2), (y_mm, 1, 3)],
            (0, 4): [(b_ilv, 1, 2, copy_s)],
            (1, 0): [(zi_quant, 0), (x_turn, 1, 0, copy_s), (x_turn, 1, 1, copy_s)],
            (1, 1): [(b_quant, 0, 2), (x_turn, 1, 2, copy_s), (x_turn, 1, 3, copy_s)],
            (1, 2): [(zt_quant, 0), (d_widen, 0, 0), (d_widen, 0, 1)],
            (1, 3): [(b_quant, 1, 2), (y_mm, 2, 0), (y_mm, 2, 1), (y_mm, 2, 2), (y_mm, 2, 3)],
            (1, 4): [(d_widen, 0, 2), (d_widen, 0, 3)],
            (2, 0): [(zi_quant, 1), (x_quant, 1, 0)],
            (2, 1): [(x_quant, 1, 1), (d_ilv, 0, 0, copy_s)],
            (2, 2): [(zt_quant, 1), (y_mm, 3, 0), (y_mm, 3, 1), (y_mm, 3, 2), (d_ilv, 0, 1, copy_s)],
            (2, 3): [(y_mm, 3, 3)],
            (2, 4): [(d_widen, 1, 0), (d_widen, 1, 1)],
            (3, 0): [(zi_quant, 2), (y_mm, 4, 0), (d_widen, 1, 2), (d_widen, 1, 3)],
            (3, 1): [(d_quant, 0), (y_mm, 4, 1)],
            (3, 2): [(zt_quant, 2), (y_mm, 4, 2), (d_ilv, 1, 0, copy_s)],
            (3, 3): [(d_ilv, 1, 1, copy_s), (y_mm, 4, 3), (d_widen, 2, 0), (d_widen, 2, 1)],
            (3, 4): [(a_turn, 0), (a_turn, 1), (a_turn, 2), (a_turn, 3), (d_widen, 2, 2), (d_widen, 2, 3)],
            (4, 0): [(zi_quant, 3), (y_mm, 5, 0)],
            (4, 1): [(a_quant,), (y_mm, 5, 1), (d_ilv, 2, 0, copy_s)],
            (4, 2): [(zt_quant, 3), (y_mm, 5, 2), (code_mm, 0, 0), (code_mm, 0, 1)],
            (4, 3): [(d_quant, 1), (y_mm, 5, 3), (code_mm, 0, 2), (code_mm, 0, 3)],
            (4, 4): [(d_ilv, 2, 1, copy_s)],
            (5, 0): [(zi_quant, 4), (code_turn, 0, 0), (code_turn, 0, 1)],
            (5, 1): [(code_v, 0, 0), (code_v, 0, 1), (code_turn, 0, 2), (code_turn, 0, 3), (code_mm, 1, 0), (code_mm, 1, 1)],
            (5, 2): [(zt_quant, 4), (code_v, 0, 2), (code_v, 0, 3), (code_mm, 1, 2), (code_mm, 1, 3)],
            (5, 3): [(d_quant, 2), (code_turn, 1, 0), (code_turn, 1, 1), (clean_mm, 0, 0, (0, 1, 2)), (clean_mm, 0, 1, (0, 1, 2)), (code_v, 1, 0)],
            (5, 4): [(code_v, 1, 1), (clean_v, 0, 0), (clean_v, 0, 1), (zi_quant, 5), (clean_mm, 0, 2, (0, 1, 2)), (clean_mm, 0, 3, (0, 1, 2))],
        }
        for k in range(6):
            for t in range(4):
                soft_ab(k, t)
                for f in plan[k, t]:
                    f[0](*f[1:])
            soft_z(k)
            for t in range(4):
                z_turn(k, t)
            for f in plan[k, 4]:
                f[0](*f[1:])

        code_turn(1, 2)
        code_turn(1, 3)
        clean_v(0, 2)
        clean_v(0, 3)
        for j in range(4, 8):
            clean_mm(0, j, (0, 1, 2), psy, "y")
        code_v(1, 2)
        code_v(1, 3)
        zt_quant(5)
        for nb in range(4):
            code_mm(2, nb)
        for j in range(4):
            clean_v(0, 4 + j)
            clean_mm(1, j, (0, 1, 2), psy, "y")
        for i in range(4):
            code_turn(2, i)
            clean_v(1, 2 * i)
            if i < 2:
                clean_mm(1, 4 + 2 * i, (0, 1, 2), psy, "y")
            clean_v(1, 2 * i + 1)
            if i < 2:
                clean_mm(1, 5 + 2 * i, (0, 1, 2), psy, "y")
            code_v(2, i)
